import numpy as np
import ml_dtypes


def mxq(x, axis, fmt="e4m3"):
    dtype, down = {"e4m3": (ml_dtypes.float8_e4m3fn, 7), "e5m2": (ml_dtypes.float8_e5m2, 14)}[fmt]
    v = np.moveaxis(np.asarray(x, np.float32).astype(ml_dtypes.bfloat16).astype(np.float64), axis, -1)
    blocks = v.reshape(v.shape[:-1] + (-1, 32))
    amax = np.abs(blocks).max(-1, keepdims=True)
    byte = np.maximum(np.where(amax > 0, np.frexp(amax)[1] - 1 + 127, 0) - down, 1)
    scale = np.exp2(byte - 127.0)
    codes = (blocks / scale).astype(np.float32).astype(dtype).astype(np.float64)
    return np.moveaxis((codes * scale).reshape(v.shape), -1, axis)


WIDE = False


def mx_kscale(k):
    if not WIDE:
        return np.ones(k)
    levels = np.array([10, -10, 5, -5, 0])
    if k % 512:
        return np.exp2(np.random.permutation(np.resize(levels, k // 32))).repeat(32)
    a = np.empty((k // 512, 16))
    for p in range(k // 512):
        a[p, :8] = np.random.permutation(np.resize(levels, 8))
        for g in range(8):
            far = levels[np.abs(levels - a[p, g]) >= 10]
            a[p, g + 8] = far[np.random.randint(len(far))]
    return np.exp2(a.ravel()).repeat(32)


def f64(x):
    return np.asarray(x).astype(np.float64)


def striped(idx):
    return np.tile(idx.reshape(-1, 16).T, (8, 1)).astype(np.uint16)


def unstriped(offs):
    return offs[:16].T.reshape(-1).astype(np.int64)


K, T, E, C, N = 1024, 512, 8, 128, 512
M = 256


def by_expert(wq, xq):
    return np.concatenate([wq[e].T @ xq[:, e * C:(e + 1) * C] for e in range(E)], axis=1)


def setup_inputs():
    n = np.random.standard_normal
    s = mx_kscale(K)[:, None]
    v = mx_kscale(N)
    first = np.random.permutation(np.repeat(np.arange(E), T // E))
    second = (first + 1 + np.random.permutation(np.repeat(np.arange(E - 1), -(-T // (E - 1)))[:T])) % E
    while np.bincount(second, minlength=E).max() != T // E:
        load = np.bincount(second, minlength=E); hi, lo = int(load.argmax()), int(load.argmin())
        t = np.flatnonzero((second == hi) & (first != lo))[0]; second[t] = lo
    slot_token = np.empty(E * C, np.int64); pos = np.empty((2, T), np.int64); fill = np.zeros(E, np.int64)
    place = np.stack([np.random.permutation(C) for _ in range(E)])
    for r, deal in enumerate((first, second)):
        for t in np.random.permutation(T):
            e = deal[t]; j = e * C + place[e, fill[e]]; fill[e] += 1; slot_token[j] = t; pos[r, t] = j
    g = np.random.uniform(0.2, 0.8, T)
    return {
        "xT": (n((K, T)) * s).astype(np.float32),
        "w": (n((E, K, N)) / np.sqrt(K) / s[None] * v[None, None, :]).astype(np.float32),
        "b": (0.3 * n((N, E)) * v[:, None]).astype(np.float32),
        "wp": (n((N, M)) / np.sqrt(N) / v[:, None]).astype(np.float32),
        "gate": np.stack([np.tile(g, (N, 1)), np.tile(1.0 - g, (N, 1))]).astype(np.float32),
        "offs": striped(slot_token),
        "pos1": striped(pos[0]),
        "pos2": striped(pos[1]),
    }


def reference(xT, w, b, wp, gate, offs, pos1, pos2):
    idx = unstriped(offs)
    xq = mxq(f64(xT)[:, idx], 0, "e4m3")
    y = by_expert(mxq(f64(w), 1, "e4m3"), xq)
    y = y + np.repeat(f64(b), C, axis=1)
    c = f64(gate[0]) * y[:, unstriped(pos1)] + f64(gate[1]) * y[:, unstriped(pos2)]
    return mxq(f64(wp), 0, "e4m3").T @ mxq(c, 0, "e4m3")

@@ -1,0 +1,320 @@
+from contextlib import ExitStack
+
+import concourse.mybir as mybir
+from concourse.masks import make_identity
+
+K, T, E, C, N, M = 1024, 512, 8, 128, 512, 256
+SLOTS = E * C
+FLOPS = 2 * SLOTS * K * N + 2 * T * N * M
+BYTES = 4 * (K * T + E * K * N + N * E + N * M + 2 * T + M * T) + 2 * 128 * (64 + 32 + 32)
+
+F32 = mybir.dt.float32
+BF16 = mybir.dt.bfloat16
+U32 = mybir.dt.uint32
+U16 = mybir.dt.uint16
+U8 = mybir.dt.uint8
+FP8X4 = mybir.dt.float8_e4m3fn_x4
+MULT = mybir.AluOpType.mult
+ADD = mybir.AluOpType.add
+IDENTITY = mybir.ActivationFunctionType.Identity
+
+P = 128
+PACK = 4
+PASSES = K // 512
+R = N // P
+HALF = T // 2
+V_COLS = dict(enumerate([0, 0, 128, 128, 128, 128, 128, 128, 64] + [0] * 11))
+X_PIECES = [[(0, 256), (256, 512)], [(0, 512)]]
+X_CASTS = [[("v", 0, 160), ("s", 160, 256), ("v", 256, 416), ("s", 416, 512)], [("v", 0, 128), ("s", 128, 512)]]
+MID = 6
+TURN = "vvvs"
+CUTS = [(0, 384), (384, 768), (768, 1024)]
+PIECES = [(0, 256), (256, 512)]
+BACK = "vsvs"
+OUTC = ["vs", "vs", "vs"]
+TAIL = "g0 g1 t0 b0 t1 q0 b1 p0 q1 p1"
+AFTER = (8, 9, 17)
+
+
+def tile_moe_nxt_lin_bias_kernel(
+    tc, xT, w, b, wp, gate, offs, pos1, pos2, out
+):
+    nc = tc.nc
+    with ExitStack() as ctx:
+        held = ctx.enter_context(tc.tile_pool(name="held", bufs=1))
+        raws = ctx.enter_context(tc.tile_pool(name="raws", bufs=12))
+        mid = ctx.enter_context(tc.tile_pool(name="mid", bufs=MID))
+        packed = ctx.enter_context(tc.tile_pool(name="packed", bufs=6))
+        prods = ctx.enter_context(tc.tile_pool(name="prods", bufs=3))
+        ypsum = ctx.enter_context(tc.psum_pool(name="ypsum", bufs=3))
+        t1psum = ctx.enter_context(tc.psum_pool(name="t1psum", bufs=1))
+        t2psum = ctx.enter_context(tc.psum_pool(name="t2psum", bufs=2))
+        opsum = ctx.enter_context(tc.psum_pool(name="opsum", bufs=1))
+
+        offs_sb = held.tile([P, SLOTS // 16], U16, name="offs_sb")
+        pos_sb = [held.tile([P, T // 16], U16, name=f"pos_sb{i}") for i in range(2)]
+        x_scale = held.tile([P, T], U8, name="x_scale", align_bytes=64)
+        nc.gpsimd.memset(x_scale[:], 0)
+        ident = held.tile([P, P], F32, name="ident")
+        make_identity(nc, ident[:])
+
+        x_raw = [held.tile([P, PACK, T], F32, name=f"x_raw{a}") for a in range(PASSES)]
+        b_sb = held.tile([P, R, E], F32, name="b_sb")
+        wp_raw = held.tile([P, PACK, M], F32, name="wp_raw")
+        gate_sb = [held.tile([P, T], F32, name=f"gate_sb{i}") for i in range(2)]
+
+        x_words = [held.tile([P, T], U32, name=f"x_words{a}", align_bytes=64) for a in range(PASSES)]
+        g_words = [held.tile([P, SLOTS], U32, name=f"g_words{a}", align_bytes=64) for a in range(PASSES)]
+        g_scale = held.tile([P, SLOTS], U8, name="g_scale", align_bytes=64)
+        x_bf = [held.tile([P, T * PACK], BF16, name=f"x_bf{a}", align_bytes=64) for a in range(PASSES)]
+        cuts = CUTS
+
+        def load_x(a):
+            rows = xT[a * 512 : (a + 1) * 512, :].rearrange("(p j) t -> p j t", j=PACK)
+            for lo, hi in X_PIECES[a]:
+                nc.sync.dma_start(out=x_raw[a][:, :, lo:hi], in_=rows[:, :, lo:hi])
+
+
+        def cast(engine_copy, grouped, raw):
+            engine_copy(
+                out=grouped.rearrange("p (c i j) -> p c j i", i=4, j=PACK),
+                in_=raw.rearrange("p j (c i) -> p c j i", i=4),
+            )
+
+        def cast_x(a):
+            for eng, lo, hi in X_CASTS[a]:
+                cast(
+                    nc.vector.tensor_copy if eng == "v" else nc.scalar.copy,
+                    x_bf[a][:, lo * PACK : hi * PACK],
+                    x_raw[a][:, :, lo:hi],
+                )
+
+        def quant_x(a):
+            nc.vector.quantize_mx(
+                out=x_words[a][:].bitcast(FP8X4), scales=x_scale[4 * a : P, :], in_=x_bf[a][:]
+            )
+
+        def gather_words(a, cut):
+            lo, hi = cuts[cut]
+            idx = offs_sb[:, lo // 16 : hi // 16]
+            nc.vector.tensor_copy(out=g_words[a][:, lo:hi], in_=x_words[a][:].indirect(idx))
+
+        def gather_scales(cut):
+            lo, hi = cuts[cut]
+            idx = offs_sb[:, lo // 16 : hi // 16]
+            nc.vector.tensor_copy(out=g_scale[:, lo:hi], in_=x_scale[:].indirect(idx))
+
+        def load_w(unit):
+            e, c0, cw = unit
+            raw = raws.tile([P, PASSES, PACK, cw], F32, name="w_raw")
+            for a in range(PASSES):
+                nc.sync.dma_start(
+                    out=raw[:, a],
+                    in_=w[e, a * 512 : (a + 1) * 512, c0 : c0 + cw].rearrange("(p j) n -> p j n", j=PACK),
+                )
+            return raw
+
+        def cast_w(unit, raw, v):
+            cw = unit[2]
+            grouped = mid.tile([P, PASSES, cw * PACK], BF16, name="w_bf", align_bytes=64)
+            cast(nc.scalar.copy, grouped[:, 0, :], raw[:, 0])
+            if v:
+                cast(nc.vector.tensor_copy, grouped[:, 1, : v * PACK], raw[:, 1, :, :v])
+            if v < cw:
+                cast(nc.scalar.copy, grouped[:, 1, v * PACK :], raw[:, 1, :, v:])
+            return grouped
+
+        def quant_w(unit, grouped):
+            cw = unit[2]
+            codes = packed.tile([P, PASSES, cw], U32, name="w_codes", align_bytes=64)
+            scales = packed.tile([P, PASSES, cw], U8, name="w_scales", align_bytes=64)
+            nc.vector.quantize_mx(
+                out=codes[:].rearrange("p a c -> p (a c)").bitcast(FP8X4),
+                scales=scales[:].rearrange("p a c -> p (a c)"),
+                in_=grouped[:].rearrange("p a c -> p (a c)"),
+            )
+            return codes, scales
+
+        y = [held.tile([P, SLOTS], F32, name=f"y{r}") for r in range(R)]
+
+        def multiply(unit, codes, scales, banks, place):
+            e, c0, cw = unit
+            cols = slice(e * C, (e + 1) * C)
+            for k in range(cw // P):
+                for a in range(PASSES):
+                    nc.tensor.matmul_mx(
+                        out=banks[k][:, place, :],
+                        lhsT=codes[:, a, k * P : (k + 1) * P].bitcast(FP8X4),
+                        lhsT_scale=scales[:, a, k * P : (k + 1) * P],
+                        rhs=g_words[a][:, cols].bitcast(FP8X4),
+                        rhs_scale=g_scale[4 * a : P, cols],
+                        start=(a == 0),
+                        stop=(a == PASSES - 1),
+                    )
+
+        def evict(group, banks):
+            e0, c0, cw = group[0]
+            n = len(group)
+            for k in range(cw // P):
+                r = c0 // P + k
+                nc.vector.tensor_tensor(
+                    y[r][:, e0 * C : (e0 + n) * C].rearrange("p (e c) -> p e c", e=n),
+                    banks[k][:],
+                    b_sb[:, r, e0 : e0 + n].unsqueeze(2).to_broadcast([P, n, C]),
+                    ADD,
+                )
+
+        wp_codes = held.tile([P, M], U32, name="wp_codes", align_bytes=64)
+        wp_scales = held.tile([P, M], U8, name="wp_scales", align_bytes=64)
+        wp_bf = held.tile([P, M * PACK], BF16, name="wp_bf", align_bytes=64)
+        cT = held.tile([P, T // P, N], BF16, name="cT", align_bytes=64)
+
+        def gather_y(r, lo, hi):
+            out_tiles = []
+            for i in range(2):
+                g = prods.tile([P, hi - lo], F32, name=f"prod{i}")
+                nc.vector.tensor_tensor(
+                    g[:], y[r][:].indirect(pos_sb[i][:, lo // 16 : hi // 16]), gate_sb[i][:, lo:hi], MULT
+                )
+                out_tiles.append(g)
+            return out_tiles
+
+        def turn(r, lo, hi, g):
+            blocks = (hi - lo) // P
+            t1 = t1psum.tile([P, blocks, P], F32, name="t1")
+            for k in range(blocks):
+                for i in range(2):
+                    nc.tensor.matmul(
+                        t1[:, k, :],
+                        g[i][:, k * P : (k + 1) * P],
+                        ident[:],
+                        start=(i == 0),
+                        stop=(i == 1),
+                        is_transpose=True,
+                    )
+            return t1
+
+        def turned(r, lo, hi, t1):
+            copy = nc.vector.tensor_copy if TURN[r] == "v" else nc.scalar.copy
+            copy(out=cT[:, lo // P : hi // P, r * P : (r + 1) * P], in_=t1[:])
+
+        groups = [
+            [(e, 0, 256) for e in range(0, 4)],
+            [(e, 0, 256) for e in range(4, 8)],
+            [(e, 256, 256) for e in range(0, 4)],
+            [(e, 256, 128) for e in range(4, 8)],
+            [(e, 384, 128) for e in range(4, 7)],
+            [(e, 384, 128) for e in range(7, 8)],
+        ]
+        load_x(0)
+        nc.sync.dma_start(offs_sb[:], offs)
+        load_x(1)
+        nc.sync.dma_start(out=b_sb[:], in_=b.rearrange("(r p) e -> p r e", p=P))
+        cast_x(0)
+        cast_x(1)
+        quant_x(0)
+        quant_x(1)
+        gather_words(0, 0)
+        gather_words(1, 0)
+        gather_scales(0)
+        later = [
+            lambda: gather_words(0, 1),
+            lambda: (gather_words(1, 1), gather_scales(1)),
+            lambda: gather_words(0, 2),
+            lambda: (gather_words(1, 2), gather_scales(2)),
+        ]
+        step = 0
+        pending = {}
+        for gi, group in enumerate(groups):
+            banks = [ypsum.tile([P, len(group), C], F32, name="acc") for k in range(group[0][2] // P)]
+            for place, unit in enumerate(group):
+                raw = load_w(unit)
+                grouped = cast_w(unit, raw, V_COLS[step])
+                if step == 5:
+                    for i in range(2):
+                        nc.sync.dma_start(pos_sb[i][:], (pos1, pos2)[i])
+                        nc.sync.dma_start(out=gate_sb[i][:], in_=gate[i, 0:P, :])
+                if step == 9:
+                    nc.sync.dma_start(out=wp_raw[:], in_=wp.rearrange("(p j) f -> p j f", j=PACK))
+                codes, scales = quant_w(unit, grouped)
+                if later:
+                    later.pop(0)()
+                multiply(unit, codes, scales, banks, place)
+                if step == 11:
+                    cast(nc.scalar.copy, wp_bf[:], wp_raw[:])
+                    nc.vector.quantize_mx(out=wp_codes[:].bitcast(FP8X4), scales=wp_scales[:], in_=wp_bf[:])
+                for job in pending.pop(step, []):
+                    job()
+                step += 1
+            evict(group, banks)
+            if gi == 1:
+                for r in range(2):
+                    def first(r=r):
+                        t1 = turn(r, 0, T, gather_y(r, 0, T))
+                        pending.setdefault(step + 1, []).append(lambda: turned(r, 0, T, t1))
+                    pending.setdefault(AFTER[r], []).append(first)
+            if gi == 3:
+                def second():
+                    t1 = turn(2, 0, T, gather_y(2, 0, T))
+                    pending.setdefault(step + 1, []).append(lambda: turned(2, 0, T, t1))
+                pending.setdefault(AFTER[2], []).append(second)
+        for key in sorted(pending):
+            for job in pending[key]:
+                job()
+
+        c_tiles = []
+        for k, (lo, hi) in enumerate(PIECES):
+            n = hi - lo
+            c_tiles.append((
+                held.tile([P, n * PACK], BF16, name=f"c_bf{k}", align_bytes=64),
+                held.tile([P, n], U32, name=f"c_codes{k}", align_bytes=64),
+                held.tile([P, n], U8, name=f"c_scales{k}", align_bytes=64),
+                held.tile([P, 2, n], F32, name=f"staged{k}"),
+            ))
+
+        def turn_back(k):
+            lo, hi = PIECES[k]
+            for i, block in enumerate(range(lo // P, hi // P)):
+                words = cT[:, block, :].bitcast(F32)
+                t2 = t2psum.tile([P, 2, P], F32, name="t2")
+                for u in range(2):
+                    nc.tensor.transpose(t2[:, u, :], words[:, u : N // 2 : 2], ident[:])
+                dst = c_tiles[k][0][:, i * P * PACK : (i + 1) * P * PACK].bitcast(F32)
+                copy = nc.vector.tensor_copy if BACK[block] == "v" else nc.scalar.copy
+                copy(out=dst.rearrange("p (t u) -> p t u", u=2), in_=t2[:].rearrange("p u t -> p t u"))
+
+        def quant_c(k):
+            c_bf, codes, scales, staged = c_tiles[k]
+            nc.vector.quantize_mx(out=codes[:].bitcast(FP8X4), scales=scales[:], in_=c_bf[:])
+
+        def project(k):
+            lo, hi = PIECES[k]
+            c_bf, codes, scales, staged = c_tiles[k]
+            for f in range(2):
+                acc = opsum.tile([P, hi - lo], F32, name=f"out_acc{f}")
+                nc.tensor.matmul_mx(
+                    out=acc[:],
+                    lhsT=wp_codes[:, f * P : (f + 1) * P].bitcast(FP8X4),
+                    lhsT_scale=wp_scales[:, f * P : (f + 1) * P],
+                    rhs=codes[:].bitcast(FP8X4),
+                    rhs_scale=scales[:],
+                    start=True,
+                    stop=True,
+                )
+                copy = nc.vector.tensor_copy if OUTC[k][f] == "v" else nc.scalar.copy
+                copy(out=staged[:, f, :], in_=acc[:])
+            nc.sync.dma_start(out=out.rearrange("(f p) t -> p f t", p=P)[:, :, lo:hi], in_=staged[:])
+
+        last = {}
+        for op in TAIL.split():
+            k = int(op[1])
+            if op[0] == "g":
+                last[k] = gather_y(3, *PIECES[k])
+            elif op[0] == "t":
+                turned(3, *PIECES[k], turn(3, *PIECES[k], last[k]))
+            elif op[0] == "b":
+                turn_back(k)
+            elif op[0] == "q":
+                quant_c(k)
+            else:
+                project(k)

@@ -1,7 +1,6 @@
 from contextlib import ExitStack
 
 import concourse.mybir as mybir
-from concourse.masks import make_identity
 
 K, T, E, C, N, M = 1024, 512, 8, 128, 512, 256
 SLOTS = E * C
@@ -23,17 +22,22 @@ PACK = 4
 PASSES = K // 512
 R = N // P
 HALF = T // 2
-V_COLS = dict(enumerate([0, 0, 128, 128, 128, 128, 128, 128, 64] + [0] * 11))
-X_PIECES = [[(0, 256), (256, 512)], [(0, 512)]]
-X_CASTS = [[("v", 0, 160), ("s", 160, 256), ("v", 256, 416), ("s", 416, 512)], [("v", 0, 128), ("s", 128, 512)]]
-MID = 6
-TURN = "vvvs"
-CUTS = [(0, 384), (384, 768), (768, 1024)]
-PIECES = [(0, 256), (256, 512)]
-BACK = "vsvs"
-OUTC = ["vs", "vs", "vs"]
-TAIL = "g0 g1 t0 b0 t1 q0 b1 p0 q1 p1"
-AFTER = (8, 9, 17)
+V_M = [16, 48, 16, 48, 48, 64, 64, 32, 32, 32, 48, 64, 48, 64, 96, 96]
+PIECE_Q = [1] * 15 + [4]
+X_PIECES = [[(0, 512)], [(0, 512)]]
+X_CASTS = [[("v", 0, 352), ("s", 352, 512)], [("s", 0, 512)]]
+MID = 4
+RAWS = 12
+CODES = 6
+CUTS = [(0, 256), (256, 640), (640, 1024)]
+PIECES = [(0, 256), (256, 384), (384, 512)]
+OUTC = ["ss", "vs", "vs"]
+TAIL = "f0 f1 f2 h0 a0 h1 q0 a1 h2 p0 q1 a2 p1 q2 p2"
+DMA_AT = {"pos1": 15, "pos2": 15, "gate0": 15, "gate1": 15, "wp": 15}
+WP_ENG = "s"
+WP_AT = 15
+EVICTS = [(0, 4, "v"), (4, 2, "v"), (6, 2, "s")]
+BIG = 0
 
 
 def tile_moe_nxt_lin_bias_kernel(
@@ -42,21 +46,15 @@ def tile_moe_nxt_lin_bias_kernel(
     nc = tc.nc
     with ExitStack() as ctx:
         held = ctx.enter_context(tc.tile_pool(name="held", bufs=1))
-        raws = ctx.enter_context(tc.tile_pool(name="raws", bufs=12))
+        raws = ctx.enter_context(tc.tile_pool(name="raws", bufs=RAWS))
         mid = ctx.enter_context(tc.tile_pool(name="mid", bufs=MID))
-        packed = ctx.enter_context(tc.tile_pool(name="packed", bufs=6))
-        prods = ctx.enter_context(tc.tile_pool(name="prods", bufs=3))
-        ypsum = ctx.enter_context(tc.psum_pool(name="ypsum", bufs=3))
-        t1psum = ctx.enter_context(tc.psum_pool(name="t1psum", bufs=1))
-        t2psum = ctx.enter_context(tc.psum_pool(name="t2psum", bufs=2))
-        opsum = ctx.enter_context(tc.psum_pool(name="opsum", bufs=1))
+        packed = ctx.enter_context(tc.tile_pool(name="packed", bufs=CODES))
+        banks_pool = ctx.enter_context(tc.psum_pool(name="banks", bufs=1))
 
         offs_sb = held.tile([P, SLOTS // 16], U16, name="offs_sb")
         pos_sb = [held.tile([P, T // 16], U16, name=f"pos_sb{i}") for i in range(2)]
         x_scale = held.tile([P, T], U8, name="x_scale", align_bytes=64)
         nc.gpsimd.memset(x_scale[:], 0)
-        ident = held.tile([P, P], F32, name="ident")
-        make_identity(nc, ident[:])
 
         x_raw = [held.tile([P, PACK, T], F32, name=f"x_raw{a}") for a in range(PASSES)]
         b_sb = held.tile([P, R, E], F32, name="b_sb")
@@ -104,164 +102,78 @@ def tile_moe_nxt_lin_bias_kernel(
             idx = offs_sb[:, lo // 16 : hi // 16]
             nc.vector.tensor_copy(out=g_scale[:, lo:hi], in_=x_scale[:].indirect(idx))
 
-        def load_w(unit):
-            e, c0, cw = unit
-            raw = raws.tile([P, PASSES, PACK, cw], F32, name="w_raw")
-            for a in range(PASSES):
-                nc.sync.dma_start(
-                    out=raw[:, a],
-                    in_=w[e, a * 512 : (a + 1) * 512, c0 : c0 + cw].rearrange("(p j) n -> p j n", j=PACK),
-                )
-            return raw
+        raw_of = {}
 
-        def cast_w(unit, raw, v):
-            cw = unit[2]
-            grouped = mid.tile([P, PASSES, cw * PACK], BF16, name="w_bf", align_bytes=64)
-            cast(nc.scalar.copy, grouped[:, 0, :], raw[:, 0])
+        def load_w(step):
+            e, a = divmod(step, PASSES)
+            if step < BIG:
+                if a == 0:
+                    raw = raws.tile([P, PASSES, PACK, N], F32, name="w_raw2", bufs=4)
+                    nc.sync.dma_start(
+                        out=raw[:].rearrange("p a j n -> p a (j n)"),
+                        in_=w[e].rearrange("(a p j) n -> p a (j n)", a=PASSES, j=PACK),
+                    )
+                    raw_of[e] = raw
+                return raw_of[e][:, a]
+            raw = raws.tile([P, PACK, N], F32, name="w_raw", bufs=RAWS)
+            nc.sync.dma_start(out=raw[:], in_=w[e, a * 512 : (a + 1) * 512, :].rearrange("(p j) n -> p j n", j=PACK))
+            return raw[:]
+
+        def cast_w(step, raw):
+            v = V_M[step]
+            grouped = mid.tile([P, N * PACK], BF16, name="w_bf", align_bytes=64)
+            dst = grouped[:].rearrange("p (t m j) -> p m j t", t=R, j=PACK)
+            src = raw.rearrange("p j (m t) -> p m j t", t=R)
             if v:
-                cast(nc.vector.tensor_copy, grouped[:, 1, : v * PACK], raw[:, 1, :, :v])
-            if v < cw:
-                cast(nc.scalar.copy, grouped[:, 1, v * PACK :], raw[:, 1, :, v:])
+                nc.vector.tensor_copy(out=dst[:, :v], in_=src[:, :v])
+            if v < P:
+                nc.scalar.copy(out=dst[:, v:], in_=src[:, v:])
             return grouped
 
-        def quant_w(unit, grouped):
-            cw = unit[2]
-            codes = packed.tile([P, PASSES, cw], U32, name="w_codes", align_bytes=64)
-            scales = packed.tile([P, PASSES, cw], U8, name="w_scales", align_bytes=64)
-            nc.vector.quantize_mx(
-                out=codes[:].rearrange("p a c -> p (a c)").bitcast(FP8X4),
-                scales=scales[:].rearrange("p a c -> p (a c)"),
-                in_=grouped[:].rearrange("p a c -> p (a c)"),
-            )
-            return codes, scales
+        def quant_w(step, grouped, codes, scales):
+            n = PIECE_Q[step]
+            for i in range(n):
+                lo, hi = i * N // n, (i + 1) * N // n
+                nc.vector.quantize_mx(
+                    out=codes[:, lo:hi].bitcast(FP8X4), scales=scales[:, lo:hi], in_=grouped[:, lo * PACK : hi * PACK]
+                )
 
         y = [held.tile([P, SLOTS], F32, name=f"y{r}") for r in range(R)]
 
-        def multiply(unit, codes, scales, banks, place):
-            e, c0, cw = unit
+        def multiply(e, quantised, bank_of):
             cols = slice(e * C, (e + 1) * C)
-            for k in range(cw // P):
+            for r in range(R):
+                bank, place = bank_of(r, e)
                 for a in range(PASSES):
+                    codes, scales = quantised[a]
                     nc.tensor.matmul_mx(
-                        out=banks[k][:, place, :],
-                        lhsT=codes[:, a, k * P : (k + 1) * P].bitcast(FP8X4),
-                        lhsT_scale=scales[:, a, k * P : (k + 1) * P],
+                        out=bank[:, place, :],
+                        lhsT=codes[:, r * P : (r + 1) * P].bitcast(FP8X4),
+                        lhsT_scale=scales[:, r * P : (r + 1) * P],
                         rhs=g_words[a][:, cols].bitcast(FP8X4),
                         rhs_scale=g_scale[4 * a : P, cols],
                         start=(a == 0),
                         stop=(a == PASSES - 1),
                     )
 
-        def evict(group, banks):
-            e0, c0, cw = group[0]
-            n = len(group)
-            for k in range(cw // P):
-                r = c0 // P + k
+        def evict(r, e0, n, bank, eng):
+            if eng == "v":
                 nc.vector.tensor_tensor(
                     y[r][:, e0 * C : (e0 + n) * C].rearrange("p (e c) -> p e c", e=n),
-                    banks[k][:],
+                    bank[:],
                     b_sb[:, r, e0 : e0 + n].unsqueeze(2).to_broadcast([P, n, C]),
                     ADD,
                 )
+            else:
+                for i in range(n):
+                    nc.scalar.activation(
+                        y[r][:, (e0 + i) * C : (e0 + i + 1) * C], bank[:, i, :], IDENTITY, bias=b_sb[:, r, e0 + i : e0 + i + 1]
+                    )
 
         wp_codes = held.tile([P, M], U32, name="wp_codes", align_bytes=64)
         wp_scales = held.tile([P, M], U8, name="wp_scales", align_bytes=64)
         wp_bf = held.tile([P, M * PACK], BF16, name="wp_bf", align_bytes=64)
-        cT = held.tile([P, T // P, N], BF16, name="cT", align_bytes=64)
-
-        def gather_y(r, lo, hi):
-            out_tiles = []
-            for i in range(2):
-                g = prods.tile([P, hi - lo], F32, name=f"prod{i}")
-                nc.vector.tensor_tensor(
-                    g[:], y[r][:].indirect(pos_sb[i][:, lo // 16 : hi // 16]), gate_sb[i][:, lo:hi], MULT
-                )
-                out_tiles.append(g)
-            return out_tiles
-
-        def turn(r, lo, hi, g):
-            blocks = (hi - lo) // P
-            t1 = t1psum.tile([P, blocks, P], F32, name="t1")
-            for k in range(blocks):
-                for i in range(2):
-                    nc.tensor.matmul(
-                        t1[:, k, :],
-                        g[i][:, k * P : (k + 1) * P],
-                        ident[:],
-                        start=(i == 0),
-                        stop=(i == 1),
-                        is_transpose=True,
-                    )
-            return t1
-
-        def turned(r, lo, hi, t1):
-            copy = nc.vector.tensor_copy if TURN[r] == "v" else nc.scalar.copy
-            copy(out=cT[:, lo // P : hi // P, r * P : (r + 1) * P], in_=t1[:])
-
-        groups = [
-            [(e, 0, 256) for e in range(0, 4)],
-            [(e, 0, 256) for e in range(4, 8)],
-            [(e, 256, 256) for e in range(0, 4)],
-            [(e, 256, 128) for e in range(4, 8)],
-            [(e, 384, 128) for e in range(4, 7)],
-            [(e, 384, 128) for e in range(7, 8)],
-        ]
-        load_x(0)
-        nc.sync.dma_start(offs_sb[:], offs)
-        load_x(1)
-        nc.sync.dma_start(out=b_sb[:], in_=b.rearrange("(r p) e -> p r e", p=P))
-        cast_x(0)
-        cast_x(1)
-        quant_x(0)
-        quant_x(1)
-        gather_words(0, 0)
-        gather_words(1, 0)
-        gather_scales(0)
-        later = [
-            lambda: gather_words(0, 1),
-            lambda: (gather_words(1, 1), gather_scales(1)),
-            lambda: gather_words(0, 2),
-            lambda: (gather_words(1, 2), gather_scales(2)),
-        ]
-        step = 0
-        pending = {}
-        for gi, group in enumerate(groups):
-            banks = [ypsum.tile([P, len(group), C], F32, name="acc") for k in range(group[0][2] // P)]
-            for place, unit in enumerate(group):
-                raw = load_w(unit)
-                grouped = cast_w(unit, raw, V_COLS[step])
-                if step == 5:
-                    for i in range(2):
-                        nc.sync.dma_start(pos_sb[i][:], (pos1, pos2)[i])
-                        nc.sync.dma_start(out=gate_sb[i][:], in_=gate[i, 0:P, :])
-                if step == 9:
-                    nc.sync.dma_start(out=wp_raw[:], in_=wp.rearrange("(p j) f -> p j f", j=PACK))
-                codes, scales = quant_w(unit, grouped)
-                if later:
-                    later.pop(0)()
-                multiply(unit, codes, scales, banks, place)
-                if step == 11:
-                    cast(nc.scalar.copy, wp_bf[:], wp_raw[:])
-                    nc.vector.quantize_mx(out=wp_codes[:].bitcast(FP8X4), scales=wp_scales[:], in_=wp_bf[:])
-                for job in pending.pop(step, []):
-                    job()
-                step += 1
-            evict(group, banks)
-            if gi == 1:
-                for r in range(2):
-                    def first(r=r):
-                        t1 = turn(r, 0, T, gather_y(r, 0, T))
-                        pending.setdefault(step + 1, []).append(lambda: turned(r, 0, T, t1))
-                    pending.setdefault(AFTER[r], []).append(first)
-            if gi == 3:
-                def second():
-                    t1 = turn(2, 0, T, gather_y(2, 0, T))
-                    pending.setdefault(step + 1, []).append(lambda: turned(2, 0, T, t1))
-                pending.setdefault(AFTER[2], []).append(second)
-        for key in sorted(pending):
-            for job in pending[key]:
-                job()
-
+        prod = [held.tile([P, R, T], F32, name=f"prod{i}") for i in range(2)]
         c_tiles = []
         for k, (lo, hi) in enumerate(PIECES):
             n = hi - lo
@@ -272,16 +184,20 @@ def tile_moe_nxt_lin_bias_kernel(
                 held.tile([P, 2, n], F32, name=f"staged{k}"),
             ))
 
-        def turn_back(k):
+        def gather_y(r, lo, hi):
+            for i in range(2):
+                nc.vector.tensor_tensor(
+                    prod[i][:, r, lo:hi], y[r][:].indirect(pos_sb[i][:, lo // 16 : hi // 16]), gate_sb[i][:, lo:hi], MULT
+                )
+
+        def combine(k):
             lo, hi = PIECES[k]
-            for i, block in enumerate(range(lo // P, hi // P)):
-                words = cT[:, block, :].bitcast(F32)
-                t2 = t2psum.tile([P, 2, P], F32, name="t2")
-                for u in range(2):
-                    nc.tensor.transpose(t2[:, u, :], words[:, u : N // 2 : 2], ident[:])
-                dst = c_tiles[k][0][:, i * P * PACK : (i + 1) * P * PACK].bitcast(F32)
-                copy = nc.vector.tensor_copy if BACK[block] == "v" else nc.scalar.copy
-                copy(out=dst.rearrange("p (t u) -> p t u", u=2), in_=t2[:].rearrange("p u t -> p t u"))
+            nc.vector.tensor_tensor(
+                c_tiles[k][0][:].rearrange("p (c i r) -> p c r i", i=4, r=R),
+                prod[0][:, :, lo:hi].rearrange("p r (c i) -> p c r i", i=4),
+                prod[1][:, :, lo:hi].rearrange("p r (c i) -> p c r i", i=4),
+                ADD,
+            )
 
         def quant_c(k):
             c_bf, codes, scales, staged = c_tiles[k]
@@ -291,7 +207,7 @@ def tile_moe_nxt_lin_bias_kernel(
             lo, hi = PIECES[k]
             c_bf, codes, scales, staged = c_tiles[k]
             for f in range(2):
-                acc = opsum.tile([P, hi - lo], F32, name=f"out_acc{f}")
+                acc = banks_pool.tile([P, hi - lo], F32, name=f"out_acc{f}", bufs=1)
                 nc.tensor.matmul_mx(
                     out=acc[:],
                     lhsT=wp_codes[:, f * P : (f + 1) * P].bitcast(FP8X4),
@@ -305,15 +221,72 @@ def tile_moe_nxt_lin_bias_kernel(
                 copy(out=staged[:, f, :], in_=acc[:])
             nc.sync.dma_start(out=out.rearrange("(f p) t -> p f t", p=P)[:, :, lo:hi], in_=staged[:])
 
-        last = {}
+        load_x(0)
+        nc.sync.dma_start(offs_sb[:], offs)
+        load_x(1)
+        nc.sync.dma_start(out=b_sb[:], in_=b.rearrange("(p r) e -> p r e", r=R))
+        cast_x(0)
+        cast_x(1)
+        quant_x(0)
+        quant_x(1)
+        gather_words(0, 0)
+        gather_words(1, 0)
+        gather_scales(0)
+        later = [
+            lambda: gather_words(0, 1),
+            lambda: (gather_words(1, 1), gather_scales(1)),
+            lambda: gather_words(0, 2),
+            lambda: (gather_words(1, 2), gather_scales(2)),
+        ]
+        open_banks = {}
+
+        def bank_of(r, e):
+            for gi, (e0, n, eng) in enumerate(EVICTS):
+                if e0 <= e < e0 + n:
+                    if (gi, r) not in open_banks:
+                        open_banks[gi, r] = banks_pool.tile([P, n, C], F32, name="acc", bufs=6)
+                    return open_banks[gi, r], e - e0
+
+        quantised = {}
+        for step in range(E * PASSES):
+            e, a = divmod(step, PASSES)
+            raw = load_w(step)
+            grouped = cast_w(step, raw)
+            for key, at in DMA_AT.items():
+                if at == step:
+                    if key == "wp":
+                        nc.sync.dma_start(out=wp_raw[:], in_=wp.rearrange("(p j) f -> p j f", j=PACK))
+                    elif key[:3] == "pos":
+                        i = int(key[3]) - 1
+                        nc.sync.dma_start(pos_sb[i][:], (pos1, pos2)[i])
+                    else:
+                        i = int(key[4])
+                        nc.sync.dma_start(out=gate_sb[i][:], in_=gate[i, 0:P, :])
+            quantised[a] = (
+                packed.tile([P, N], U32, name="w_codes", align_bytes=64),
+                packed.tile([P, N], U8, name="w_scales", align_bytes=64),
+            )
+            quant_w(step, grouped, *quantised[a])
+            if later:
+                later.pop(0)()
+            if a == PASSES - 1:
+                multiply(e, quantised, bank_of)
+                for gi, (e0, n, eng) in enumerate(EVICTS):
+                    if e == e0 + n - 1:
+                        for r in range(R):
+                            evict(r, e0, n, open_banks.pop((gi, r)), eng)
+            if step == WP_AT:
+                cast({"s": nc.scalar.copy, "v": nc.vector.tensor_copy, "p": nc.gpsimd.tensor_copy}[WP_ENG], wp_bf[:], wp_raw[:])
+                nc.vector.quantize_mx(out=wp_codes[:].bitcast(FP8X4), scales=wp_scales[:], in_=wp_bf[:])
+
         for op in TAIL.split():
             k = int(op[1])
-            if op[0] == "g":
-                last[k] = gather_y(3, *PIECES[k])
-            elif op[0] == "t":
-                turned(3, *PIECES[k], turn(3, *PIECES[k], last[k]))
-            elif op[0] == "b":
-                turn_back(k)
+            if op[0] == "f":
+                gather_y(k, 0, T)
+            elif op[0] == "h":
+                gather_y(R - 1, *PIECES[k])
+            elif op[0] == "a":
+                combine(k)
             elif op[0] == "q":
                 quant_c(k)
             else:

@@ -22,7 +22,6 @@ PACK = 4
 PASSES = K // 512
 R = N // P
 HALF = T // 2
-V_M = [16, 48, 16, 48, 48, 64, 64, 32, 32, 32, 48, 64, 48, 64, 96, 96]
 PIECE_Q = [1] * 15 + [4]
 X_PIECES = [[(0, 512)], [(0, 512)]]
 X_CASTS = [[("v", 0, 352), ("s", 352, 512)], [("s", 0, 512)]]
@@ -31,13 +30,15 @@ RAWS = 12
 CODES = 6
 CUTS = [(0, 256), (256, 640), (640, 1024)]
 PIECES = [(0, 256), (256, 384), (384, 512)]
-OUTC = ["ss", "vs", "vs"]
+OUTC = ["ss", "ss", "vs"]
 TAIL = "f0 f1 f2 h0 a0 h1 q0 a1 h2 p0 q1 a2 p1 q2 p2"
 DMA_AT = {"pos1": 15, "pos2": 15, "gate0": 15, "gate1": 15, "wp": 15}
 WP_ENG = "s"
 WP_AT = 15
 EVICTS = [(0, 4, "v"), (4, 2, "v"), (6, 2, "s")]
-BIG = 0
+B_AT = 3
+V_T = [1, 2] * 7 + [2] * 2
+SPLIT_T = [0] * 15 + [1]
 
 
 def tile_moe_nxt_lin_bias_kernel(
@@ -102,32 +103,20 @@ def tile_moe_nxt_lin_bias_kernel(
             idx = offs_sb[:, lo // 16 : hi // 16]
             nc.vector.tensor_copy(out=g_scale[:, lo:hi], in_=x_scale[:].indirect(idx))
 
-        raw_of = {}
-
         def load_w(step):
             e, a = divmod(step, PASSES)
-            if step < BIG:
-                if a == 0:
-                    raw = raws.tile([P, PASSES, PACK, N], F32, name="w_raw2", bufs=4)
-                    nc.sync.dma_start(
-                        out=raw[:].rearrange("p a j n -> p a (j n)"),
-                        in_=w[e].rearrange("(a p j) n -> p a (j n)", a=PASSES, j=PACK),
-                    )
-                    raw_of[e] = raw
-                return raw_of[e][:, a]
             raw = raws.tile([P, PACK, N], F32, name="w_raw", bufs=RAWS)
             nc.sync.dma_start(out=raw[:], in_=w[e, a * 512 : (a + 1) * 512, :].rearrange("(p j) n -> p j n", j=PACK))
             return raw[:]
 
         def cast_w(step, raw):
-            v = V_M[step]
             grouped = mid.tile([P, N * PACK], BF16, name="w_bf", align_bytes=64)
-            dst = grouped[:].rearrange("p (t m j) -> p m j t", t=R, j=PACK)
-            src = raw.rearrange("p j (m t) -> p m j t", t=R)
-            if v:
-                nc.vector.tensor_copy(out=dst[:, :v], in_=src[:, :v])
-            if v < P:
-                nc.scalar.copy(out=dst[:, v:], in_=src[:, v:])
+            dst = grouped[:].rearrange("p (t h i j) -> p t h j i", t=R, i=4, j=PACK)
+            src = raw.rearrange("p j (h t i) -> p t h j i", t=R, i=4)
+            for copy, lo, hi in ((nc.vector.tensor_copy, 0, V_T[step]), (nc.scalar.copy, V_T[step], R)):
+                for a, b in [(t, t + 1) for t in range(lo, hi)] if SPLIT_T[step] else [(lo, hi)]:
+                    if a < b:
+                        copy(out=dst[:, a:b], in_=src[:, a:b])
             return grouped
 
         def quant_w(step, grouped, codes, scales):
@@ -224,7 +213,6 @@ def tile_moe_nxt_lin_bias_kernel(
         load_x(0)
         nc.sync.dma_start(offs_sb[:], offs)
         load_x(1)
-        nc.sync.dma_start(out=b_sb[:], in_=b.rearrange("(p r) e -> p r e", r=R))
         cast_x(0)
         cast_x(1)
         quant_x(0)
@@ -251,11 +239,15 @@ def tile_moe_nxt_lin_bias_kernel(
         for step in range(E * PASSES):
             e, a = divmod(step, PASSES)
             raw = load_w(step)
+            if step == B_AT:
+                for i in range(4):
+                    nc.sync.dma_start(out=b_sb[i:P:4], in_=b.rearrange("(h r i) e -> i h r e", r=R, i=4)[i])
             grouped = cast_w(step, raw)
             for key, at in DMA_AT.items():
                 if at == step:
                     if key == "wp":
-                        nc.sync.dma_start(out=wp_raw[:], in_=wp.rearrange("(p j) f -> p j f", j=PACK))
+                        for i in range(4):
+                            nc.sync.dma_start(out=wp_raw[i:P:4], in_=wp.rearrange("(h j i) f -> i h j f", j=PACK, i=4)[i])
                     elif key[:3] == "pos":
                         i = int(key[3]) - 1
                         nc.sync.dma_start(pos_sb[i][:], (pos1, pos2)[i])

@@ -4,8 +4,9 @@ import concourse.mybir as mybir
 
 K, T, E, C, N, M = 1024, 512, 8, 128, 512, 256
 SLOTS = E * C
+
 FLOPS = 2 * SLOTS * K * N + 2 * T * N * M
-BYTES = 4 * (K * T + E * K * N + N * E + N * M + 2 * T + M * T) + 2 * 128 * (64 + 32 + 32)
+BYTES = 4 * (K * T + E * K * N + N * E + N * M + 2 * T + M * T) + 2 * 8 * 16 * (SLOTS + 2 * T) // 16
 
 F32 = mybir.dt.float32
 BF16 = mybir.dt.bfloat16
@@ -19,26 +20,27 @@ IDENTITY = mybir.ActivationFunctionType.Identity
 
 P = 128
 PACK = 4
-PASSES = K // 512
+K_PASS = P * PACK
+PASSES = K // K_PASS
 R = N // P
-HALF = T // 2
-PIECE_Q = [1] * 15 + [4]
-X_PIECES = [[(0, 512)], [(0, 512)]]
-X_CASTS = [[("v", 0, 352), ("s", 352, 512)], [("s", 0, 512)]]
-MID = 4
-RAWS = 12
-CODES = 6
-CUTS = [(0, 256), (256, 640), (640, 1024)]
-PIECES = [(0, 256), (256, 384), (384, 512)]
-OUTC = ["ss", "ss", "vs"]
-TAIL = "f0 f1 f2 h0 a0 h1 q0 a1 h2 p0 q1 a2 p1 q2 p2"
-DMA_AT = {"pos1": 15, "pos2": 15, "gate0": 15, "gate1": 15, "wp": 15}
-WP_ENG = "s"
-WP_AT = 15
-EVICTS = [(0, 4, "v"), (4, 2, "v"), (6, 2, "s")]
-B_AT = 3
-V_T = [1, 2] * 7 + [2] * 2
-SPLIT_T = [0] * 15 + [1]
+LINE = 4
+SLABS = E * PASSES
+
+X_TOKENS_VECTOR = 352
+W_COLUMNS_VECTOR = [48] * (SLABS - 2) + [80] * 2
+
+SLOT_PIECES = [(0, 256), (256, 640), (640, 1024)]
+
+EXPERT_GROUPS = [(0, 4, "vector"), (4, 2, "vector"), (6, 2, "scalar")]
+
+TOKEN_PIECES = [(0, 256), (256, 384), (384, 512)]
+
+
+def interleave(grouped, raw):
+    return (
+        grouped.rearrange("p (c i j) -> p c j i", i=LINE, j=PACK),
+        raw.rearrange("p j (c i) -> p c j i", i=LINE),
+    )
 
 
 def tile_moe_nxt_lin_bias_kernel(
@@ -47,239 +49,210 @@ def tile_moe_nxt_lin_bias_kernel(
     nc = tc.nc
     with ExitStack() as ctx:
         held = ctx.enter_context(tc.tile_pool(name="held", bufs=1))
-        raws = ctx.enter_context(tc.tile_pool(name="raws", bufs=RAWS))
-        mid = ctx.enter_context(tc.tile_pool(name="mid", bufs=MID))
-        packed = ctx.enter_context(tc.tile_pool(name="packed", bufs=CODES))
-        banks_pool = ctx.enter_context(tc.psum_pool(name="banks", bufs=1))
+        slab_pool = ctx.enter_context(tc.tile_pool(name="slab_pool", bufs=12))
+        cast_pool = ctx.enter_context(tc.tile_pool(name="cast_pool", bufs=4))
+        code_pool = ctx.enter_context(tc.tile_pool(name="code_pool", bufs=6))
+        banks = ctx.enter_context(tc.psum_pool(name="banks", bufs=1))
 
         offs_sb = held.tile([P, SLOTS // 16], U16, name="offs_sb")
         pos_sb = [held.tile([P, T // 16], U16, name=f"pos_sb{i}") for i in range(2)]
-        x_scale = held.tile([P, T], U8, name="x_scale", align_bytes=64)
-        nc.gpsimd.memset(x_scale[:], 0)
+
+        x_scales = held.tile([P, T], U8, name="x_scales", align_bytes=64)
+        nc.gpsimd.memset(x_scales[:], 0)
 
         x_raw = [held.tile([P, PACK, T], F32, name=f"x_raw{a}") for a in range(PASSES)]
+        x_cast = [held.tile([P, T * PACK], BF16, name=f"x_cast{a}", align_bytes=64) for a in range(PASSES)]
+        x_codes = [held.tile([P, T], U32, name=f"x_codes{a}", align_bytes=64) for a in range(PASSES)]
+        slot_codes = [held.tile([P, SLOTS], U32, name=f"slot_codes{a}", align_bytes=64) for a in range(PASSES)]
+        slot_scales = held.tile([P, SLOTS], U8, name="slot_scales", align_bytes=64)
         b_sb = held.tile([P, R, E], F32, name="b_sb")
-        wp_raw = held.tile([P, PACK, M], F32, name="wp_raw")
         gate_sb = [held.tile([P, T], F32, name=f"gate_sb{i}") for i in range(2)]
-
-        x_words = [held.tile([P, T], U32, name=f"x_words{a}", align_bytes=64) for a in range(PASSES)]
-        g_words = [held.tile([P, SLOTS], U32, name=f"g_words{a}", align_bytes=64) for a in range(PASSES)]
-        g_scale = held.tile([P, SLOTS], U8, name="g_scale", align_bytes=64)
-        x_bf = [held.tile([P, T * PACK], BF16, name=f"x_bf{a}", align_bytes=64) for a in range(PASSES)]
-        cuts = CUTS
-
-        def load_x(a):
-            rows = xT[a * 512 : (a + 1) * 512, :].rearrange("(p j) t -> p j t", j=PACK)
-            for lo, hi in X_PIECES[a]:
-                nc.sync.dma_start(out=x_raw[a][:, :, lo:hi], in_=rows[:, :, lo:hi])
-
-
-        def cast(engine_copy, grouped, raw):
-            engine_copy(
-                out=grouped.rearrange("p (c i j) -> p c j i", i=4, j=PACK),
-                in_=raw.rearrange("p j (c i) -> p c j i", i=4),
-            )
-
-        def cast_x(a):
-            for eng, lo, hi in X_CASTS[a]:
-                cast(
-                    nc.vector.tensor_copy if eng == "v" else nc.scalar.copy,
-                    x_bf[a][:, lo * PACK : hi * PACK],
-                    x_raw[a][:, :, lo:hi],
-                )
-
-        def quant_x(a):
-            nc.vector.quantize_mx(
-                out=x_words[a][:].bitcast(FP8X4), scales=x_scale[4 * a : P, :], in_=x_bf[a][:]
-            )
-
-        def gather_words(a, cut):
-            lo, hi = cuts[cut]
-            idx = offs_sb[:, lo // 16 : hi // 16]
-            nc.vector.tensor_copy(out=g_words[a][:, lo:hi], in_=x_words[a][:].indirect(idx))
-
-        def gather_scales(cut):
-            lo, hi = cuts[cut]
-            idx = offs_sb[:, lo // 16 : hi // 16]
-            nc.vector.tensor_copy(out=g_scale[:, lo:hi], in_=x_scale[:].indirect(idx))
-
-        def load_w(step):
-            e, a = divmod(step, PASSES)
-            raw = raws.tile([P, PACK, N], F32, name="w_raw", bufs=RAWS)
-            nc.sync.dma_start(out=raw[:], in_=w[e, a * 512 : (a + 1) * 512, :].rearrange("(p j) n -> p j n", j=PACK))
-            return raw[:]
-
-        def cast_w(step, raw):
-            grouped = mid.tile([P, N * PACK], BF16, name="w_bf", align_bytes=64)
-            dst = grouped[:].rearrange("p (t h i j) -> p t h j i", t=R, i=4, j=PACK)
-            src = raw.rearrange("p j (h t i) -> p t h j i", t=R, i=4)
-            for copy, lo, hi in ((nc.vector.tensor_copy, 0, V_T[step]), (nc.scalar.copy, V_T[step], R)):
-                for a, b in [(t, t + 1) for t in range(lo, hi)] if SPLIT_T[step] else [(lo, hi)]:
-                    if a < b:
-                        copy(out=dst[:, a:b], in_=src[:, a:b])
-            return grouped
-
-        def quant_w(step, grouped, codes, scales):
-            n = PIECE_Q[step]
-            for i in range(n):
-                lo, hi = i * N // n, (i + 1) * N // n
-                nc.vector.quantize_mx(
-                    out=codes[:, lo:hi].bitcast(FP8X4), scales=scales[:, lo:hi], in_=grouped[:, lo * PACK : hi * PACK]
-                )
-
+        wp_raw = held.tile([P, PACK, M], F32, name="wp_raw")
+        wp_cast = held.tile([P, M * PACK], BF16, name="wp_cast", align_bytes=64)
+        wp_codes = held.tile([P, M], U32, name="wp_codes", align_bytes=64)
+        wp_scales = held.tile([P, M], U8, name="wp_scales", align_bytes=64)
         y = [held.tile([P, SLOTS], F32, name=f"y{r}") for r in range(R)]
 
-        def multiply(e, quantised, bank_of):
-            cols = slice(e * C, (e + 1) * C)
+        def load_x(a):
+            rows = xT[a * K_PASS : (a + 1) * K_PASS, :]
+            nc.sync.dma_start(out=x_raw[a][:], in_=rows.rearrange("(p j) t -> p j t", j=PACK))
+
+        def quantise_x(a):
+            nc.vector.quantize_mx(
+                out=x_codes[a][:].bitcast(FP8X4), scales=x_scales[4 * a : P, :], in_=x_cast[a][:]
+            )
+
+        def gather_codes(a, slot_piece):
+            lo, hi = SLOT_PIECES[slot_piece]
+            offsets = offs_sb[:, lo // 16 : hi // 16]
+            nc.vector.tensor_copy(out=slot_codes[a][:, lo:hi], in_=x_codes[a][:].indirect(offsets))
+
+        def gather_scales(slot_piece):
+            lo, hi = SLOT_PIECES[slot_piece]
+            offsets = offs_sb[:, lo // 16 : hi // 16]
+            nc.vector.tensor_copy(out=slot_scales[:, lo:hi], in_=x_scales[:].indirect(offsets))
+
+        def load_slab(slab):
+            e, a = divmod(slab, PASSES)
+            raw = slab_pool.tile([P, PACK, N], F32, name="w_raw")
+            rows = w[e, a * K_PASS : (a + 1) * K_PASS, :]
+            nc.sync.dma_start(out=raw[:], in_=rows.rearrange("(p j) n -> p j n", j=PACK))
+            return raw
+
+        def cast_slab(slab, raw):
+            grouped = cast_pool.tile([P, N * PACK], BF16, name="w_cast", align_bytes=64)
+            dst = grouped[:].rearrange("p (r m j) -> p m j r", r=R, j=PACK)
+            src = raw[:].rearrange("p j (m r) -> p m j r", r=R)
+            split = W_COLUMNS_VECTOR[slab]
+            parts = 2 if slab == SLABS - 1 else 1
+            for copy, lo, hi in ((nc.vector.tensor_copy, 0, split), (nc.scalar.copy, split, P)):
+                for part in range(parts):
+                    rs = slice(part * R // parts, (part + 1) * R // parts)
+                    copy(out=dst[:, lo:hi, :, rs], in_=src[:, lo:hi, :, rs])
+            return grouped
+
+        def quantise_slab(slab, grouped):
+            codes = code_pool.tile([P, N], U32, name="w_codes", align_bytes=64)
+            scales = code_pool.tile([P, N], U8, name="w_scales", align_bytes=64)
+            parts = R if slab == SLABS - 1 else 1
+            for part in range(parts):
+                lo, hi = part * N // parts, (part + 1) * N // parts
+                nc.vector.quantize_mx(
+                    out=codes[:, lo:hi].bitcast(FP8X4),
+                    scales=scales[:, lo:hi],
+                    in_=grouped[:, lo * PACK : hi * PACK],
+                )
+            return codes, scales
+
+        def multiply(e, slabs, group_banks, place):
+            slots = slice(e * C, (e + 1) * C)
             for r in range(R):
-                bank, place = bank_of(r, e)
-                for a in range(PASSES):
-                    codes, scales = quantised[a]
+                for a, (codes, scales) in enumerate(slabs):
                     nc.tensor.matmul_mx(
-                        out=bank[:, place, :],
+                        out=group_banks[r][:, place, :],
                         lhsT=codes[:, r * P : (r + 1) * P].bitcast(FP8X4),
                         lhsT_scale=scales[:, r * P : (r + 1) * P],
-                        rhs=g_words[a][:, cols].bitcast(FP8X4),
-                        rhs_scale=g_scale[4 * a : P, cols],
+                        rhs=slot_codes[a][:, slots].bitcast(FP8X4),
+                        rhs_scale=slot_scales[4 * a : P, slots],
                         start=(a == 0),
                         stop=(a == PASSES - 1),
                     )
 
-        def evict(r, e0, n, bank, eng):
-            if eng == "v":
-                nc.vector.tensor_tensor(
-                    y[r][:, e0 * C : (e0 + n) * C].rearrange("p (e c) -> p e c", e=n),
-                    bank[:],
-                    b_sb[:, r, e0 : e0 + n].unsqueeze(2).to_broadcast([P, n, C]),
-                    ADD,
-                )
-            else:
-                for i in range(n):
-                    nc.scalar.activation(
-                        y[r][:, (e0 + i) * C : (e0 + i + 1) * C], bank[:, i, :], IDENTITY, bias=b_sb[:, r, e0 + i : e0 + i + 1]
+        def copy_out(first, experts, engine, group_banks):
+            for r in range(R):
+                if engine == "vector":
+                    results = y[r][:, first * C : (first + experts) * C]
+                    bias = b_sb[:, r, first : first + experts].unsqueeze(2).to_broadcast([P, experts, C])
+                    nc.vector.tensor_tensor(
+                        results.rearrange("p (e c) -> p e c", e=experts), group_banks[r][:], bias, ADD
                     )
-
-        wp_codes = held.tile([P, M], U32, name="wp_codes", align_bytes=64)
-        wp_scales = held.tile([P, M], U8, name="wp_scales", align_bytes=64)
-        wp_bf = held.tile([P, M * PACK], BF16, name="wp_bf", align_bytes=64)
-        prod = [held.tile([P, R, T], F32, name=f"prod{i}") for i in range(2)]
-        c_tiles = []
-        for k, (lo, hi) in enumerate(PIECES):
-            n = hi - lo
-            c_tiles.append((
-                held.tile([P, n * PACK], BF16, name=f"c_bf{k}", align_bytes=64),
-                held.tile([P, n], U32, name=f"c_codes{k}", align_bytes=64),
-                held.tile([P, n], U8, name=f"c_scales{k}", align_bytes=64),
-                held.tile([P, 2, n], F32, name=f"staged{k}"),
-            ))
-
-        def gather_y(r, lo, hi):
-            for i in range(2):
-                nc.vector.tensor_tensor(
-                    prod[i][:, r, lo:hi], y[r][:].indirect(pos_sb[i][:, lo // 16 : hi // 16]), gate_sb[i][:, lo:hi], MULT
-                )
-
-        def combine(k):
-            lo, hi = PIECES[k]
-            nc.vector.tensor_tensor(
-                c_tiles[k][0][:].rearrange("p (c i r) -> p c r i", i=4, r=R),
-                prod[0][:, :, lo:hi].rearrange("p r (c i) -> p c r i", i=4),
-                prod[1][:, :, lo:hi].rearrange("p r (c i) -> p c r i", i=4),
-                ADD,
-            )
-
-        def quant_c(k):
-            c_bf, codes, scales, staged = c_tiles[k]
-            nc.vector.quantize_mx(out=codes[:].bitcast(FP8X4), scales=scales[:], in_=c_bf[:])
-
-        def project(k):
-            lo, hi = PIECES[k]
-            c_bf, codes, scales, staged = c_tiles[k]
-            for f in range(2):
-                acc = banks_pool.tile([P, hi - lo], F32, name=f"out_acc{f}", bufs=1)
-                nc.tensor.matmul_mx(
-                    out=acc[:],
-                    lhsT=wp_codes[:, f * P : (f + 1) * P].bitcast(FP8X4),
-                    lhsT_scale=wp_scales[:, f * P : (f + 1) * P],
-                    rhs=codes[:].bitcast(FP8X4),
-                    rhs_scale=scales[:],
-                    start=True,
-                    stop=True,
-                )
-                copy = nc.vector.tensor_copy if OUTC[k][f] == "v" else nc.scalar.copy
-                copy(out=staged[:, f, :], in_=acc[:])
-            nc.sync.dma_start(out=out.rearrange("(f p) t -> p f t", p=P)[:, :, lo:hi], in_=staged[:])
+                else:
+                    for i in range(experts):
+                        e = first + i
+                        nc.scalar.activation(
+                            y[r][:, e * C : (e + 1) * C],
+                            group_banks[r][:, i, :],
+                            IDENTITY,
+                            bias=b_sb[:, r, e : e + 1],
+                        )
 
         load_x(0)
         nc.sync.dma_start(offs_sb[:], offs)
         load_x(1)
-        cast_x(0)
-        cast_x(1)
-        quant_x(0)
-        quant_x(1)
-        gather_words(0, 0)
-        gather_words(1, 0)
+        nc.sync.dma_start(out=b_sb[:], in_=b.rearrange("(p r) e -> p r e", r=R))
+
+        dst, src = interleave(x_cast[0][:], x_raw[0][:])
+        split = X_TOKENS_VECTOR // LINE
+        nc.vector.tensor_copy(out=dst[:, :split], in_=src[:, :split])
+        nc.scalar.copy(out=dst[:, split:], in_=src[:, split:])
+        dst, src = interleave(x_cast[1][:], x_raw[1][:])
+        nc.scalar.copy(out=dst, in_=src)
+        for a in range(PASSES):
+            quantise_x(a)
+        for a in range(PASSES):
+            gather_codes(a, 0)
         gather_scales(0)
-        later = [
-            lambda: gather_words(0, 1),
-            lambda: (gather_words(1, 1), gather_scales(1)),
-            lambda: gather_words(0, 2),
-            lambda: (gather_words(1, 2), gather_scales(2)),
-        ]
-        open_banks = {}
 
-        def bank_of(r, e):
-            for gi, (e0, n, eng) in enumerate(EVICTS):
-                if e0 <= e < e0 + n:
-                    if (gi, r) not in open_banks:
-                        open_banks[gi, r] = banks_pool.tile([P, n, C], F32, name="acc", bufs=6)
-                    return open_banks[gi, r], e - e0
+        for first, experts, engine in EXPERT_GROUPS:
+            group_banks = []
+            for place in range(experts):
+                e = first + place
+                slabs = []
+                for a in range(PASSES):
+                    slab = e * PASSES + a
+                    grouped = cast_slab(slab, load_slab(slab))
+                    if slab == SLABS - 1:
+                        for i, pos in enumerate((pos1, pos2)):
+                            nc.sync.dma_start(pos_sb[i][:], pos)
+                        for i in range(2):
+                            nc.sync.dma_start(out=gate_sb[i][:], in_=gate[i, 0:P, :])
+                        nc.sync.dma_start(out=wp_raw[:], in_=wp.rearrange("(p j) f -> p j f", j=PACK))
+                    slabs.append(quantise_slab(slab, grouped))
+                    slot_piece = 1 + e
+                    if slot_piece < len(SLOT_PIECES):
+                        gather_codes(a, slot_piece)
+                        if a == PASSES - 1:
+                            gather_scales(slot_piece)
+                if place == 0:
+                    group_banks = [banks.tile([P, experts, C], F32, name="y_bank", bufs=6) for r in range(R)]
+                multiply(e, slabs, group_banks, place)
+            copy_out(first, experts, engine, group_banks)
 
-        quantised = {}
-        for step in range(E * PASSES):
-            e, a = divmod(step, PASSES)
-            raw = load_w(step)
-            if step == B_AT:
-                for i in range(4):
-                    nc.sync.dma_start(out=b_sb[i:P:4], in_=b.rearrange("(h r i) e -> i h r e", r=R, i=4)[i])
-            grouped = cast_w(step, raw)
-            for key, at in DMA_AT.items():
-                if at == step:
-                    if key == "wp":
-                        for i in range(4):
-                            nc.sync.dma_start(out=wp_raw[i:P:4], in_=wp.rearrange("(h j i) f -> i h j f", j=PACK, i=4)[i])
-                    elif key[:3] == "pos":
-                        i = int(key[3]) - 1
-                        nc.sync.dma_start(pos_sb[i][:], (pos1, pos2)[i])
-                    else:
-                        i = int(key[4])
-                        nc.sync.dma_start(out=gate_sb[i][:], in_=gate[i, 0:P, :])
-            quantised[a] = (
-                packed.tile([P, N], U32, name="w_codes", align_bytes=64),
-                packed.tile([P, N], U8, name="w_scales", align_bytes=64),
-            )
-            quant_w(step, grouped, *quantised[a])
-            if later:
-                later.pop(0)()
-            if a == PASSES - 1:
-                multiply(e, quantised, bank_of)
-                for gi, (e0, n, eng) in enumerate(EVICTS):
-                    if e == e0 + n - 1:
-                        for r in range(R):
-                            evict(r, e0, n, open_banks.pop((gi, r)), eng)
-            if step == WP_AT:
-                cast({"s": nc.scalar.copy, "v": nc.vector.tensor_copy, "p": nc.gpsimd.tensor_copy}[WP_ENG], wp_bf[:], wp_raw[:])
-                nc.vector.quantize_mx(out=wp_codes[:].bitcast(FP8X4), scales=wp_scales[:], in_=wp_bf[:])
+        dst, src = interleave(wp_cast[:], wp_raw[:])
+        nc.scalar.copy(out=dst, in_=src)
+        nc.vector.quantize_mx(out=wp_codes[:].bitcast(FP8X4), scales=wp_scales[:], in_=wp_cast[:])
 
-        for op in TAIL.split():
-            k = int(op[1])
-            if op[0] == "f":
-                gather_y(k, 0, T)
-            elif op[0] == "h":
-                gather_y(R - 1, *PIECES[k])
-            elif op[0] == "a":
-                combine(k)
-            elif op[0] == "q":
-                quant_c(k)
-            else:
-                project(k)
+        product = [held.tile([P, R, T], F32, name=f"product{i}") for i in range(2)]
+        c_cast, c_codes, c_scales, staged = [], [], [], []
+        for k, (lo, hi) in enumerate(TOKEN_PIECES):
+            c_cast.append(held.tile([P, (hi - lo) * PACK], BF16, name=f"c_cast{k}", align_bytes=64))
+            c_codes.append(held.tile([P, hi - lo], U32, name=f"c_codes{k}", align_bytes=64))
+            c_scales.append(held.tile([P, hi - lo], U8, name=f"c_scales{k}", align_bytes=64))
+            staged.append(held.tile([P, M // P, hi - lo], F32, name=f"staged{k}"))
+
+        def gather_y(r, lo, hi):
+            for i in range(2):
+                offsets = pos_sb[i][:, lo // 16 : hi // 16]
+                nc.vector.tensor_tensor(
+                    product[i][:, r, lo:hi], y[r][:].indirect(offsets), gate_sb[i][:, lo:hi], MULT
+                )
+
+        def combine(k):
+            lo, hi = TOKEN_PIECES[k]
+            dst, first_product = interleave(c_cast[k][:], product[0][:, :, lo:hi])
+            second_product = interleave(c_cast[k][:], product[1][:, :, lo:hi])[1]
+            nc.vector.tensor_tensor(dst, first_product, second_product, ADD)
+
+        def quantise_c(k):
+            nc.vector.quantize_mx(out=c_codes[k][:].bitcast(FP8X4), scales=c_scales[k][:], in_=c_cast[k][:])
+
+        def project(k):
+            lo, hi = TOKEN_PIECES[k]
+            is_last = k == len(TOKEN_PIECES) - 1
+            for f in range(M // P):
+                acc = banks.tile([P, hi - lo], F32, name=f"out_bank{f}")
+                nc.tensor.matmul_mx(
+                    out=acc[:],
+                    lhsT=wp_codes[:, f * P : (f + 1) * P].bitcast(FP8X4),
+                    lhsT_scale=wp_scales[:, f * P : (f + 1) * P],
+                    rhs=c_codes[k][:].bitcast(FP8X4),
+                    rhs_scale=c_scales[k][:],
+                    start=True,
+                    stop=True,
+                )
+                copy = nc.vector.tensor_copy if is_last and f == 0 else nc.scalar.copy
+                copy(out=staged[k][:, f, :], in_=acc[:])
+            nc.sync.dma_start(out=out.rearrange("(f p) t -> p f t", p=P)[:, :, lo:hi], in_=staged[k][:])
+
+        for r in range(R - 1):
+            gather_y(r, 0, T)
+        token_pieces = len(TOKEN_PIECES)
+        for step in range(token_pieces + 2):
+            if step < token_pieces:
+                gather_y(R - 1, *TOKEN_PIECES[step])
+            if step >= 2:
+                project(step - 2)
+            if 1 <= step <= token_pieces:
+                quantise_c(step - 1)
+            if step < token_pieces:
+                combine(step)

from contextlib import ExitStack

import concourse.mybir as mybir

K, T, E, C, N, M = 1024, 512, 8, 128, 512, 256
SLOTS = E * C

FLOPS = 2 * SLOTS * K * N + 2 * T * N * M
BYTES = 4 * (K * T + E * K * N + N * E + N * M + 2 * T + M * T) + 2 * 8 * 16 * (SLOTS + 2 * T) // 16

F32 = mybir.dt.float32
BF16 = mybir.dt.bfloat16
U32 = mybir.dt.uint32
U16 = mybir.dt.uint16
U8 = mybir.dt.uint8
FP8X4 = mybir.dt.float8_e4m3fn_x4
MULT = mybir.AluOpType.mult
ADD = mybir.AluOpType.add
IDENTITY = mybir.ActivationFunctionType.Identity

P = 128
PACK = 4
K_PASS = P * PACK
PASSES = K // K_PASS
R = N // P
LINE = 4
SLABS = E * PASSES

X_TOKENS_VECTOR = 352
W_COLUMNS_VECTOR = [48] * (SLABS - 2) + [80] * 2

SLOT_PIECES = [(0, 256), (256, 640), (640, 1024)]

EXPERT_GROUPS = [(0, 4, "vector"), (4, 2, "vector"), (6, 2, "scalar")]

TOKEN_PIECES = [(0, 256), (256, 384), (384, 512)]


def interleave(grouped, raw):
    return (
        grouped.rearrange("p (c i j) -> p c j i", i=LINE, j=PACK),
        raw.rearrange("p j (c i) -> p c j i", i=LINE),
    )


def tile_moe_nxt_lin_bias_kernel(
    tc, xT, w, b, wp, gate, offs, pos1, pos2, out
):
    nc = tc.nc
    with ExitStack() as ctx:
        held = ctx.enter_context(tc.tile_pool(name="held", bufs=1))
        slab_pool = ctx.enter_context(tc.tile_pool(name="slab_pool", bufs=12))
        cast_pool = ctx.enter_context(tc.tile_pool(name="cast_pool", bufs=4))
        code_pool = ctx.enter_context(tc.tile_pool(name="code_pool", bufs=6))
        banks = ctx.enter_context(tc.psum_pool(name="banks", bufs=1))

        offs_sb = held.tile([P, SLOTS // 16], U16, name="offs_sb")
        pos_sb = [held.tile([P, T // 16], U16, name=f"pos_sb{i}") for i in range(2)]

        x_scales = held.tile([P, T], U8, name="x_scales", align_bytes=64)
        nc.gpsimd.memset(x_scales[:], 0)

        x_raw = [held.tile([P, PACK, T], F32, name=f"x_raw{a}") for a in range(PASSES)]
        x_cast = [held.tile([P, T * PACK], BF16, name=f"x_cast{a}", align_bytes=64) for a in range(PASSES)]
        x_codes = [held.tile([P, T], U32, name=f"x_codes{a}", align_bytes=64) for a in range(PASSES)]
        slot_codes = [held.tile([P, SLOTS], U32, name=f"slot_codes{a}", align_bytes=64) for a in range(PASSES)]
        slot_scales = held.tile([P, SLOTS], U8, name="slot_scales", align_bytes=64)
        b_sb = held.tile([P, R, E], F32, name="b_sb")
        gate_sb = [held.tile([P, T], F32, name=f"gate_sb{i}") for i in range(2)]
        wp_raw = held.tile([P, PACK, M], F32, name="wp_raw")
        wp_cast = held.tile([P, M * PACK], BF16, name="wp_cast", align_bytes=64)
        wp_codes = held.tile([P, M], U32, name="wp_codes", align_bytes=64)
        wp_scales = held.tile([P, M], U8, name="wp_scales", align_bytes=64)
        y = [held.tile([P, SLOTS], F32, name=f"y{r}") for r in range(R)]

        def load_x(a):
            rows = xT[a * K_PASS : (a + 1) * K_PASS, :]
            nc.sync.dma_start(out=x_raw[a][:], in_=rows.rearrange("(p j) t -> p j t", j=PACK))

        def quantise_x(a):
            nc.vector.quantize_mx(
                out=x_codes[a][:].bitcast(FP8X4), scales=x_scales[4 * a : P, :], in_=x_cast[a][:]
            )

        def gather_codes(a, slot_piece):
            lo, hi = SLOT_PIECES[slot_piece]
            offsets = offs_sb[:, lo // 16 : hi // 16]
            nc.vector.tensor_copy(out=slot_codes[a][:, lo:hi], in_=x_codes[a][:].indirect(offsets))

        def gather_scales(slot_piece):
            lo, hi = SLOT_PIECES[slot_piece]
            offsets = offs_sb[:, lo // 16 : hi // 16]
            nc.vector.tensor_copy(out=slot_scales[:, lo:hi], in_=x_scales[:].indirect(offsets))

        def load_slab(slab):
            e, a = divmod(slab, PASSES)
            raw = slab_pool.tile([P, PACK, N], F32, name="w_raw")
            rows = w[e, a * K_PASS : (a + 1) * K_PASS, :]
            nc.sync.dma_start(out=raw[:], in_=rows.rearrange("(p j) n -> p j n", j=PACK))
            return raw

        def cast_slab(slab, raw):
            grouped = cast_pool.tile([P, N * PACK], BF16, name="w_cast", align_bytes=64)
            dst = grouped[:].rearrange("p (r m j) -> p m j r", r=R, j=PACK)
            src = raw[:].rearrange("p j (m r) -> p m j r", r=R)
            split = W_COLUMNS_VECTOR[slab]
            parts = 2 if slab == SLABS - 1 else 1
            for copy, lo, hi in ((nc.vector.tensor_copy, 0, split), (nc.scalar.copy, split, P)):
                for part in range(parts):
                    rs = slice(part * R // parts, (part + 1) * R // parts)
                    copy(out=dst[:, lo:hi, :, rs], in_=src[:, lo:hi, :, rs])
            return grouped

        def quantise_slab(slab, grouped):
            codes = code_pool.tile([P, N], U32, name="w_codes", align_bytes=64)
            scales = code_pool.tile([P, N], U8, name="w_scales", align_bytes=64)
            parts = R if slab == SLABS - 1 else 1
            for part in range(parts):
                lo, hi = part * N // parts, (part + 1) * N // parts
                nc.vector.quantize_mx(
                    out=codes[:, lo:hi].bitcast(FP8X4),
                    scales=scales[:, lo:hi],
                    in_=grouped[:, lo * PACK : hi * PACK],
                )
            return codes, scales

        def multiply(e, slabs, group_banks, place):
            slots = slice(e * C, (e + 1) * C)
            for r in range(R):
                for a, (codes, scales) in enumerate(slabs):
                    nc.tensor.matmul_mx(
                        out=group_banks[r][:, place, :],
                        lhsT=codes[:, r * P : (r + 1) * P].bitcast(FP8X4),
                        lhsT_scale=scales[:, r * P : (r + 1) * P],
                        rhs=slot_codes[a][:, slots].bitcast(FP8X4),
                        rhs_scale=slot_scales[4 * a : P, slots],
                        start=(a == 0),
                        stop=(a == PASSES - 1),
                    )

        def copy_out(first, experts, engine, group_banks):
            for r in range(R):
                if engine == "vector":
                    results = y[r][:, first * C : (first + experts) * C]
                    bias = b_sb[:, r, first : first + experts].unsqueeze(2).to_broadcast([P, experts, C])
                    nc.vector.tensor_tensor(
                        results.rearrange("p (e c) -> p e c", e=experts), group_banks[r][:], bias, ADD
                    )
                else:
                    for i in range(experts):
                        e = first + i
                        nc.scalar.activation(
                            y[r][:, e * C : (e + 1) * C],
                            group_banks[r][:, i, :],
                            IDENTITY,
                            bias=b_sb[:, r, e : e + 1],
                        )

        load_x(0)
        nc.sync.dma_start(offs_sb[:], offs)
        load_x(1)
        nc.sync.dma_start(out=b_sb[:], in_=b.rearrange("(p r) e -> p r e", r=R))

        dst, src = interleave(x_cast[0][:], x_raw[0][:])
        split = X_TOKENS_VECTOR // LINE
        nc.vector.tensor_copy(out=dst[:, :split], in_=src[:, :split])
        nc.scalar.copy(out=dst[:, split:], in_=src[:, split:])
        dst, src = interleave(x_cast[1][:], x_raw[1][:])
        nc.scalar.copy(out=dst, in_=src)
        for a in range(PASSES):
            quantise_x(a)
        for a in range(PASSES):
            gather_codes(a, 0)
        gather_scales(0)

        for first, experts, engine in EXPERT_GROUPS:
            group_banks = []
            for place in range(experts):
                e = first + place
                slabs = []
                for a in range(PASSES):
                    slab = e * PASSES + a
                    grouped = cast_slab(slab, load_slab(slab))
                    if slab == SLABS - 1:
                        for i, pos in enumerate((pos1, pos2)):
                            nc.sync.dma_start(pos_sb[i][:], pos)
                        for i in range(2):
                            nc.sync.dma_start(out=gate_sb[i][:], in_=gate[i, 0:P, :])
                        nc.sync.dma_start(out=wp_raw[:], in_=wp.rearrange("(p j) f -> p j f", j=PACK))
                    slabs.append(quantise_slab(slab, grouped))
                    slot_piece = 1 + e
                    if slot_piece < len(SLOT_PIECES):
                        gather_codes(a, slot_piece)
                        if a == PASSES - 1:
                            gather_scales(slot_piece)
                if place == 0:
                    group_banks = [banks.tile([P, experts, C], F32, name="y_bank", bufs=6) for r in range(R)]
                multiply(e, slabs, group_banks, place)
            copy_out(first, experts, engine, group_banks)

        dst, src = interleave(wp_cast[:], wp_raw[:])
        nc.scalar.copy(out=dst, in_=src)
        nc.vector.quantize_mx(out=wp_codes[:].bitcast(FP8X4), scales=wp_scales[:], in_=wp_cast[:])

        product = [held.tile([P, R, T], F32, name=f"product{i}") for i in range(2)]
        c_cast, c_codes, c_scales, staged = [], [], [], []
        for k, (lo, hi) in enumerate(TOKEN_PIECES):
            c_cast.append(held.tile([P, (hi - lo) * PACK], BF16, name=f"c_cast{k}", align_bytes=64))
            c_codes.append(held.tile([P, hi - lo], U32, name=f"c_codes{k}", align_bytes=64))
            c_scales.append(held.tile([P, hi - lo], U8, name=f"c_scales{k}", align_bytes=64))
            staged.append(held.tile([P, M // P, hi - lo], F32, name=f"staged{k}"))

        def gather_y(r, lo, hi):
            for i in range(2):
                offsets = pos_sb[i][:, lo // 16 : hi // 16]
                nc.vector.tensor_tensor(
                    product[i][:, r, lo:hi], y[r][:].indirect(offsets), gate_sb[i][:, lo:hi], MULT
                )

        def combine(k):
            lo, hi = TOKEN_PIECES[k]
            dst, first_product = interleave(c_cast[k][:], product[0][:, :, lo:hi])
            second_product = interleave(c_cast[k][:], product[1][:, :, lo:hi])[1]
            nc.vector.tensor_tensor(dst, first_product, second_product, ADD)

        def quantise_c(k):
            nc.vector.quantize_mx(out=c_codes[k][:].bitcast(FP8X4), scales=c_scales[k][:], in_=c_cast[k][:])

        def project(k):
            lo, hi = TOKEN_PIECES[k]
            is_last = k == len(TOKEN_PIECES) - 1
            for f in range(M // P):
                acc = banks.tile([P, hi - lo], F32, name=f"out_bank{f}")
                nc.tensor.matmul_mx(
                    out=acc[:],
                    lhsT=wp_codes[:, f * P : (f + 1) * P].bitcast(FP8X4),
                    lhsT_scale=wp_scales[:, f * P : (f + 1) * P],
                    rhs=c_codes[k][:].bitcast(FP8X4),
                    rhs_scale=c_scales[k][:],
                    start=True,
                    stop=True,
                )
                copy = nc.vector.tensor_copy if is_last and f == 0 else nc.scalar.copy
                copy(out=staged[k][:, f, :], in_=acc[:])
            nc.sync.dma_start(out=out.rearrange("(f p) t -> p f t", p=P)[:, :, lo:hi], in_=staged[k][:])

        for r in range(R - 1):
            gather_y(r, 0, T)
        token_pieces = len(TOKEN_PIECES)
        for step in range(token_pieces + 2):
            if step < token_pieces:
                gather_y(R - 1, *TOKEN_PIECES[step])
            if step >= 2:
                project(step - 2)
            if 1 <= step <= token_pieces:
                quantise_c(step - 1)
            if step < token_pieces:
                combine(step)
